import numpy as np
import ml_dtypes


def mxq(x, axis, fmt="e4m3"):
    dtype, down = {"e4m3": (ml_dtypes.float8_e4m3fn, 7), "e5m2": (ml_dtypes.float8_e5m2, 14)}[fmt]
    v = np.moveaxis(np.asarray(x, np.float32).astype(ml_dtypes.bfloat16).astype(np.float64), axis, -1)
    blocks = v.reshape(v.shape[:-1] + (-1, 32))
    amax = np.abs(blocks).max(-1, keepdims=True)
    byte = np.maximum(np.where(amax > 0, np.frexp(amax)[1] - 1 + 127, 0) - down, 1)
    scale = np.exp2(byte - 127.0)
    codes = (blocks / scale).astype(np.float32).astype(dtype).astype(np.float64)
    return np.moveaxis((codes * scale).reshape(v.shape), -1, axis)


WIDE = False


def mx_kscale(k):
    if not WIDE:
        return np.ones(k)
    levels = np.array([10, -10, 5, -5, 0])
    if k % 512:
        return np.exp2(np.random.permutation(np.resize(levels, k // 32))).repeat(32)
    a = np.empty((k // 512, 16))
    for p in range(k // 512):
        a[p, :8] = np.random.permutation(np.resize(levels, 8))
        for g in range(8):
            far = levels[np.abs(levels - a[p, g]) >= 10]
            a[p, g + 8] = far[np.random.randint(len(far))]
    return np.exp2(a.ravel()).repeat(32)


def f64(x):
    return np.asarray(x).astype(np.float64)


def striped(idx):
    return np.tile(idx.reshape(-1, 16).T, (8, 1)).astype(np.uint16)


def unstriped(offs):
    return offs[:16].T.reshape(-1).astype(np.int64)


def relu(v):
    return np.maximum(v, 0.0)


K, T, S, V, H, N = 1024, 1024, 768, 256, 512, 128


def setup_inputs():
    n = np.random.standard_normal
    s = mx_kscale(K)[:, None]
    u = mx_kscale(H)
    return {
        "xT": (n((K, T)) * s).astype(np.float32),
        "w1": (n((K, H)) / np.sqrt(K) / s * u).astype(np.float32),
        "w2": (n((K, H)) / np.sqrt(K) / s).astype(np.float32),
        "w3": (n((K, H)) / np.sqrt(K) / s).astype(np.float32),
        "w4": (n((H, N)) / np.sqrt(H) / u[:, None]).astype(np.float32),
        "offs": striped(np.random.permutation(T)[:S]),
    }


def reference(xT, w1, w2, w3, w4, offs):
    xq = mxq(f64(xT)[:, unstriped(offs)], 0, "e4m3")
    z = (((mxq(f64(w1), 0, "e4m3").T @ xq[:, :V])) * ((mxq(f64(w2), 0, "e4m3").T @ xq[:, V:2 * V]))) * ((mxq(f64(w3), 0, "e4m3").T @ xq[:, 2 * V:3 * V]))
    return relu(mxq(f64(w4), 0, "e4m3").T @ mxq(z, 0, "e4m3"))

@@ -1,0 +1,180 @@
+from contextlib import ExitStack
+
+import concourse.mybir as mybir
+
+K, T, V, H, N = 1024, 1024, 256, 512, 128
+PIECES = 3
+FLOPS = 2 * PIECES * K * H * V + 2 * H * N * V
+
+F32 = mybir.dt.float32
+BF16 = mybir.dt.bfloat16
+U32 = mybir.dt.uint32
+U16 = mybir.dt.uint16
+U8 = mybir.dt.uint8
+FP8X4 = mybir.dt.float8_e4m3fn_x4
+MULT = mybir.AluOpType.mult
+COPY = mybir.ActivationFunctionType.Copy
+RELU = mybir.ActivationFunctionType.Relu
+
+P = 128
+PACK = 4
+K_PASS = P * PACK
+PASSES = K // K_PASS
+T_HALF = T // 2
+V_HALF = V // 2
+LIST_COLS = V // 16
+
+X_SCALAR_COLS = 256
+W_SCALAR_SLOTS = {(0, 0): 4, (0, 1): 3, (1, 0): 2, (1, 1): 2, (2, 0): 3, (2, 1): 2}
+
+
+def tile_picked_trilin_relu_e_kernel(tc, xT, w1, w2, w3, w4, offs, out):
+    nc = tc.nc
+    weights = (w1, w2, w3)
+    with ExitStack() as ctx:
+        keep = ctx.enter_context(tc.tile_pool(name="keep", bufs=1))
+        psum = ctx.enter_context(tc.psum_pool(name="psum", bufs=1))
+
+        offsets = keep.tile([P, PIECES * LIST_COLS], U16, name="offsets")
+        x_scales = keep.tile([P, T], U8, name="x_scales", align_bytes=64)
+        nc.gpsimd.memset(x_scales[:], 0)
+
+        x_raw = {}
+        for g in range(PASSES):
+            rows = xT[g * K_PASS : (g + 1) * K_PASS, :].rearrange("(p j) c -> p j c", j=PACK)
+            for h in range(2):
+                x_raw[g, h] = keep.tile([P, PACK, T_HALF], F32, name=f"x_raw{g}{h}", align_bytes=64)
+                nc.sync.dma_start(x_raw[g, h][:], rows[:, :, h * T_HALF : (h + 1) * T_HALF])
+                if (g, h) == (0, 0):
+                    nc.sync.dma_start(offsets[:], offs)
+        w_raw = {}
+        for d in range(PIECES):
+            for g in range(PASSES):
+                w_raw[d, g] = keep.tile([P, PACK, H], F32, name=f"w_raw{d}{g}", align_bytes=64)
+                rows = weights[d][g * K_PASS : (g + 1) * K_PASS, :].rearrange("(p j) c -> p j c", j=PACK)
+                nc.sync.dma_start(w_raw[d, g][:], rows)
+        w4_raw = keep.tile([P, PACK, N], F32, name="w4_raw", align_bytes=64)
+        w4_rows = w4.rearrange("(q t i) n -> i q t n", t=PACK, i=4)
+        for i in range(4):
+            nc.sync.dma_start(w4_raw[i:P:4, :, :], w4_rows[i])
+
+        x_words = [keep.tile([P, T], U32, name=f"x_words{g}", align_bytes=64) for g in range(PASSES)]
+        picked_words = {}
+        picked_scales = {}
+
+        def round_x(g, h):
+            packed = keep.tile([P, T_HALF * PACK], BF16, name=f"x_bf{g}{h}", align_bytes=64)
+            dst = packed[:].rearrange("p (c i j) -> p c j i", i=4, j=PACK)
+            src = x_raw[g, h][:].rearrange("p j (c i) -> p c j i", i=4)
+            cut = X_SCALAR_COLS // 4
+            nc.scalar.activation(dst[:, :cut], src[:, :cut], COPY)
+            nc.vector.tensor_copy(dst[:, cut:], src[:, cut:])
+            cols = slice(h * T_HALF, (h + 1) * T_HALF)
+            nc.vector.quantize_mx(
+                out=x_words[g][:, cols].bitcast(FP8X4), scales=x_scales[4 * g : P, cols], in_=packed[:]
+            )
+
+        def gather_words(d, g):
+            picked_words[d, g] = keep.tile([P, V], U32, name=f"picked_words{d}{g}", align_bytes=64)
+            piece = offsets[:, d * LIST_COLS : (d + 1) * LIST_COLS]
+            nc.vector.tensor_copy(picked_words[d, g][:], x_words[g][:].indirect(piece))
+
+        def gather_scales(d):
+            picked_scales[d] = keep.tile([P, V], U8, name=f"picked_scales{d}", align_bytes=64)
+            piece = offsets[:, d * LIST_COLS : (d + 1) * LIST_COLS]
+            nc.vector.tensor_copy(picked_scales[d][:], x_scales[:].indirect(piece))
+
+        w_words = {}
+        w_scales = {}
+
+        def round_w(d, g, slots_a_call):
+            packed = keep.tile([P, H * PACK], BF16, name=f"w_bf{d}{g}", align_bytes=64)
+            dst = packed[:].rearrange("p (t q i j) -> p t q j i", t=PACK, i=4, j=PACK)
+            src = w_raw[d, g][:].rearrange("p j (q t i) -> p t q j i", t=PACK, i=4)
+            on_vector = PACK - W_SCALAR_SLOTS[d, g]
+            if on_vector:
+                nc.vector.tensor_copy(dst[:, :on_vector], src[:, :on_vector])
+            for t in range(on_vector, PACK):
+                nc.scalar.activation(dst[:, t], src[:, t], COPY)
+            w_words[d, g] = keep.tile([P, H], U32, name=f"w_words{d}{g}", align_bytes=64)
+            w_scales[d, g] = keep.tile([P, H], U8, name=f"w_scales{d}{g}", align_bytes=64)
+            for t in range(0, PACK, slots_a_call):
+                cols = slice(t * P, (t + slots_a_call) * P)
+                nc.vector.quantize_mx(
+                    out=w_words[d, g][:, cols].bitcast(FP8X4),
+                    scales=w_scales[d, g][:, cols],
+                    in_=packed[:, t * K_PASS : (t + slots_a_call) * K_PASS],
+                )
+
+        def product(d, h):
+            bank = psum.tile([P, PACK, V_HALF], F32, name=f"bank{d}{h}")
+            v_cols = slice(h * V_HALF, (h + 1) * V_HALF)
+            for t in range(PACK):
+                cols = slice(t * P, (t + 1) * P)
+                for g in range(PASSES):
+                    nc.tensor.matmul_mx(
+                        out=bank[:, t, :],
+                        lhsT=w_words[d, g][:, cols].bitcast(FP8X4),
+                        lhsT_scale=w_scales[d, g][:, cols],
+                        rhs=picked_words[d, g][:, v_cols].bitcast(FP8X4),
+                        rhs_scale=picked_scales[d][4 * g : P, v_cols],
+                        start=(g == 0),
+                        stop=(g == PASSES - 1),
+                    )
+            return bank[:].rearrange("p t v -> p v t")
+
+        round_x(0, 0)
+        round_x(0, 1)
+        for d in range(PIECES):
+            gather_words(d, 0)
+        round_x(1, 0)
+        round_x(1, 1)
+        for d in range(PIECES):
+            gather_words(d, 1)
+            gather_scales(d)
+
+        round_w(0, 0, 4)
+        round_w(0, 1, 4)
+        first = [keep.tile([P, V_HALF, PACK], F32, name=f"first{h}", align_bytes=64) for h in range(2)]
+        for h in range(2):
+            nc.scalar.activation(first[h][:], product(0, h), COPY)
+        round_w(1, 0, 4)
+        round_w(1, 1, 4)
+        both = [keep.tile([P, V_HALF, PACK], F32, name=f"both{h}", align_bytes=64) for h in range(2)]
+        for h in range(2):
+            nc.vector.tensor_tensor(both[h][:], product(1, h), first[h][:], MULT)
+        round_w(2, 0, 4)
+        round_w(2, 1, 1)
+
+        w4_bf = keep.tile([P, N * PACK], BF16, name="w4_bf", align_bytes=64)
+        nc.scalar.activation(
+            w4_bf[:].rearrange("p (c i j) -> p c j i", i=4, j=PACK),
+            w4_raw[:].rearrange("p j (c i) -> p c j i", i=4),
+            COPY,
+        )
+        w4_words = keep.tile([P, N], U32, name="w4_words", align_bytes=64)
+        w4_scales = keep.tile([P, N], U8, name="w4_scales", align_bytes=64)
+        nc.vector.quantize_mx(out=w4_words[:].bitcast(FP8X4), scales=w4_scales[:], in_=w4_bf[:])
+
+        z_bf = [keep.tile([P, V_HALF, PACK], BF16, name=f"z_bf{h}", align_bytes=64) for h in range(2)]
+        for h in range(2):
+            nc.vector.tensor_tensor(z_bf[h][:], product(2, h), both[h][:], MULT)
+        for h in range(2):
+            z_words = keep.tile([P, V_HALF], U32, name=f"z_words{h}", align_bytes=64)
+            z_scales = keep.tile([P, V_HALF], U8, name=f"z_scales{h}", align_bytes=64)
+            nc.vector.quantize_mx(
+                out=z_words[:].bitcast(FP8X4), scales=z_scales[:], in_=z_bf[h][:].rearrange("p v t -> p (v t)")
+            )
+            last = psum.tile([N, V_HALF], F32, name=f"last{h}")
+            nc.tensor.matmul_mx(
+                out=last[:],
+                lhsT=w4_words[:].bitcast(FP8X4),
+                lhsT_scale=w4_scales[:],
+                rhs=z_words[:].bitcast(FP8X4),
+                rhs_scale=z_scales[:],
+                start=True,
+                stop=True,
+            )
+            result = keep.tile([N, V_HALF], F32, name=f"result{h}", align_bytes=64)
+            nc.scalar.activation(result[:], last[:], RELU)
+            nc.sync.dma_start(out[:, h * V_HALF : (h + 1) * V_HALF], result[:])

@@ -1,6 +1,7 @@
 from contextlib import ExitStack
 
 import concourse.mybir as mybir
+from concourse.masks import make_identity
 
 K, T, V, H, N = 1024, 1024, 256, 512, 128
 PIECES = 3
@@ -22,150 +23,142 @@ K_PASS = P * PACK
 PASSES = K // K_PASS
 T_HALF = T // 2
 V_HALF = V // 2
+H_HALF = H // 2
 LIST_COLS = V // 16
-
-X_SCALAR_COLS = 256
-W_SCALAR_SLOTS = {(0, 0): 4, (0, 1): 3, (1, 0): 2, (1, 1): 2, (2, 0): 3, (2, 1): 2}
 
 
 def tile_picked_trilin_relu_e_kernel(tc, xT, w1, w2, w3, w4, offs, out):
     nc = tc.nc
-    weights = (w1, w2, w3)
     with ExitStack() as ctx:
         keep = ctx.enter_context(tc.tile_pool(name="keep", bufs=1))
-        psum = ctx.enter_context(tc.psum_pool(name="psum", bufs=1))
+        psum = ctx.enter_context(tc.psum_pool(name="psum", bufs=2))
 
         offsets = keep.tile([P, PIECES * LIST_COLS], U16, name="offsets")
         x_scales = keep.tile([P, T], U8, name="x_scales", align_bytes=64)
-        nc.gpsimd.memset(x_scales[:], 0)
+        nc.gpsimd.memset(x_scales[:].bitcast(U32), 0)
+        identity = keep.tile([P, P], F32, name="identity", align_bytes=64)
+        make_identity(nc, identity[:])
 
+        def load(name, matrix, g, cols):
+            rows = matrix[g * K_PASS : (g + 1) * K_PASS, :].rearrange("(p j) c -> p j c", j=PACK)
+            raw = keep.tile([P, PACK, cols.stop - cols.start], F32, name=name, align_bytes=64)
+            nc.sync.dma_start(raw[:], rows[:, :, cols])
+            return raw
+
+        def interleave(name, raw, scalar_cols):
+            width = raw.shape[2]
+            packed = keep.tile([P, width * PACK], BF16, name=name, align_bytes=64)
+            dst = packed[:].rearrange("p (c i j) -> p c j i", i=4, j=PACK)
+            src = raw.rearrange("p j (c i) -> p c j i", i=4)
+            cut = (width - scalar_cols) // 4
+            if cut:
+                nc.vector.tensor_copy(dst[:, :cut], src[:, :cut])
+            if scalar_cols:
+                nc.scalar.activation(dst[:, cut:], src[:, cut:], COPY)
+            return packed
+
+        def quantize(words, scales, packed):
+            nc.vector.quantize_mx(out=words.bitcast(FP8X4), scales=scales, in_=packed)
+
+        halves = [slice(0, T_HALF), slice(T_HALF, T)]
         x_raw = {}
         for g in range(PASSES):
-            rows = xT[g * K_PASS : (g + 1) * K_PASS, :].rearrange("(p j) c -> p j c", j=PACK)
             for h in range(2):
-                x_raw[g, h] = keep.tile([P, PACK, T_HALF], F32, name=f"x_raw{g}{h}", align_bytes=64)
-                nc.sync.dma_start(x_raw[g, h][:], rows[:, :, h * T_HALF : (h + 1) * T_HALF])
+                x_raw[g, h] = load(f"x_raw{g}{h}", xT, g, halves[h])[:]
                 if (g, h) == (0, 0):
                     nc.sync.dma_start(offsets[:], offs)
         w_raw = {}
-        for d in range(PIECES):
-            for g in range(PASSES):
-                w_raw[d, g] = keep.tile([P, PACK, H], F32, name=f"w_raw{d}{g}", align_bytes=64)
-                rows = weights[d][g * K_PASS : (g + 1) * K_PASS, :].rearrange("(p j) c -> p j c", j=PACK)
-                nc.sync.dma_start(w_raw[d, g][:], rows)
-        w4_raw = keep.tile([P, PACK, N], F32, name="w4_raw", align_bytes=64)
-        w4_rows = w4.rearrange("(q t i) n -> i q t n", t=PACK, i=4)
-        for i in range(4):
-            nc.sync.dma_start(w4_raw[i:P:4, :, :], w4_rows[i])
+        for d, matrix in enumerate((w1, w2, w3)):
+            w_raw[d, 0] = load(f"w_raw{d}0", matrix, 0, slice(0, H))
+            if d < PIECES - 1:
+                w_raw[d, 1] = load(f"w_raw{d}1", matrix, 1, slice(0, H))
+        w3_late = [load(f"w3_late{c}", w3, 1, slice(c * H_HALF, (c + 1) * H_HALF)) for c in range(2)]
+        w4_raw = load("w4_raw", w4, 0, slice(0, N))
 
         x_words = [keep.tile([P, T], U32, name=f"x_words{g}", align_bytes=64) for g in range(PASSES)]
         picked_words = {}
-        picked_scales = {}
+        for g in range(PASSES):
+            for h in range(2):
+                packed = interleave(f"x_bf{g}{h}", x_raw[g, h], (176, 176, 512, 176)[2 * g + h])
+                quantize(x_words[g][:, halves[h]], x_scales[4 * g : P, halves[h]], packed[:])
+            picked_words[g] = keep.tile([P, PIECES * V], U32, name=f"picked_words{g}", align_bytes=64)
+            nc.vector.tensor_copy(picked_words[g][:], x_words[g][:].indirect(offsets[:]))
+        picked_scales = keep.tile([P, PIECES * V], U8, name="picked_scales", align_bytes=64)
+        nc.vector.tensor_copy(picked_scales[:], x_scales[:].indirect(offsets[:]))
 
-        def round_x(g, h):
-            packed = keep.tile([P, T_HALF * PACK], BF16, name=f"x_bf{g}{h}", align_bytes=64)
-            dst = packed[:].rearrange("p (c i j) -> p c j i", i=4, j=PACK)
-            src = x_raw[g, h][:].rearrange("p j (c i) -> p c j i", i=4)
-            cut = X_SCALAR_COLS // 4
-            nc.scalar.activation(dst[:, :cut], src[:, :cut], COPY)
-            nc.vector.tensor_copy(dst[:, cut:], src[:, cut:])
-            cols = slice(h * T_HALF, (h + 1) * T_HALF)
-            nc.vector.quantize_mx(
-                out=x_words[g][:, cols].bitcast(FP8X4), scales=x_scales[4 * g : P, cols], in_=packed[:]
+        def weights(name, raw, scalar_cols):
+            width = raw.shape[2]
+            packed = interleave(name + "_bf", raw[:], scalar_cols)
+            words = keep.tile([P, width], U32, name=name + "_words", align_bytes=64)
+            scales = keep.tile([P, width], U8, name=name + "_scales", align_bytes=64)
+            quantize(words[:], scales[:], packed[:])
+            return words, scales
+
+        def one_pass(bank, d, g, h, words, scales):
+            v_cols = slice(d * V + h * V_HALF, d * V + (h + 1) * V_HALF)
+            nc.tensor.matmul_mx(
+                out=bank,
+                lhsT=picked_words[g][:, v_cols].bitcast(FP8X4),
+                lhsT_scale=picked_scales[4 * g : P, v_cols],
+                rhs=words.bitcast(FP8X4),
+                rhs_scale=scales,
+                start=(g == 0),
+                stop=(g == PASSES - 1),
             )
 
-        def gather_words(d, g):
-            picked_words[d, g] = keep.tile([P, V], U32, name=f"picked_words{d}{g}", align_bytes=64)
-            piece = offsets[:, d * LIST_COLS : (d + 1) * LIST_COLS]
-            nc.vector.tensor_copy(picked_words[d, g][:], x_words[g][:].indirect(piece))
+        def dealt(bank):
+            return bank.rearrange("v (p u e) -> v u p e", u=2, e=2)
 
-        def gather_scales(d):
-            picked_scales[d] = keep.tile([P, V], U8, name=f"picked_scales{d}", align_bytes=64)
-            piece = offsets[:, d * LIST_COLS : (d + 1) * LIST_COLS]
-            nc.vector.tensor_copy(picked_scales[d][:], x_scales[:].indirect(piece))
+        def product(d, tag, shares):
+            banks = [psum.tile([V_HALF, H], F32, name=f"bank{d}{h}", tag=tag) for h in range(2)]
+            for g in range(PASSES):
+                words, scales = weights(f"w{d}{g}", w_raw[d, g], shares[g])
+                for h in range(2):
+                    one_pass(banks[h][:], d, g, h, words[:], scales[:])
+            return banks
 
-        w_words = {}
-        w_scales = {}
-
-        def round_w(d, g, slots_a_call):
-            packed = keep.tile([P, H * PACK], BF16, name=f"w_bf{d}{g}", align_bytes=64)
-            dst = packed[:].rearrange("p (t q i j) -> p t q j i", t=PACK, i=4, j=PACK)
-            src = w_raw[d, g][:].rearrange("p j (q t i) -> p t q j i", t=PACK, i=4)
-            on_vector = PACK - W_SCALAR_SLOTS[d, g]
-            if on_vector:
-                nc.vector.tensor_copy(dst[:, :on_vector], src[:, :on_vector])
-            for t in range(on_vector, PACK):
-                nc.scalar.activation(dst[:, t], src[:, t], COPY)
-            w_words[d, g] = keep.tile([P, H], U32, name=f"w_words{d}{g}", align_bytes=64)
-            w_scales[d, g] = keep.tile([P, H], U8, name=f"w_scales{d}{g}", align_bytes=64)
-            for t in range(0, PACK, slots_a_call):
-                cols = slice(t * P, (t + slots_a_call) * P)
-                nc.vector.quantize_mx(
-                    out=w_words[d, g][:, cols].bitcast(FP8X4),
-                    scales=w_scales[d, g][:, cols],
-                    in_=packed[:, t * K_PASS : (t + slots_a_call) * K_PASS],
-                )
-
-        def product(d, h):
-            bank = psum.tile([P, PACK, V_HALF], F32, name=f"bank{d}{h}")
-            v_cols = slice(h * V_HALF, (h + 1) * V_HALF)
-            for t in range(PACK):
-                cols = slice(t * P, (t + 1) * P)
-                for g in range(PASSES):
-                    nc.tensor.matmul_mx(
-                        out=bank[:, t, :],
-                        lhsT=w_words[d, g][:, cols].bitcast(FP8X4),
-                        lhsT_scale=w_scales[d, g][:, cols],
-                        rhs=picked_words[d, g][:, v_cols].bitcast(FP8X4),
-                        rhs_scale=picked_scales[d][4 * g : P, v_cols],
-                        start=(g == 0),
-                        stop=(g == PASSES - 1),
-                    )
-            return bank[:].rearrange("p t v -> p v t")
-
-        round_x(0, 0)
-        round_x(0, 1)
-        for d in range(PIECES):
-            gather_words(d, 0)
-        round_x(1, 0)
-        round_x(1, 1)
-        for d in range(PIECES):
-            gather_words(d, 1)
-            gather_scales(d)
-
-        round_w(0, 0, 4)
-        round_w(0, 1, 4)
-        first = [keep.tile([P, V_HALF, PACK], F32, name=f"first{h}", align_bytes=64) for h in range(2)]
+        banks_a = product(0, "early", (512, 512))
+        banks = product(1, "late", (288, 176))
+        first = [keep.tile([V_HALF, 2, P, 2], F32, name=f"first{h}", align_bytes=64) for h in range(2)]
         for h in range(2):
-            nc.scalar.activation(first[h][:], product(0, h), COPY)
-        round_w(1, 0, 4)
-        round_w(1, 1, 4)
-        both = [keep.tile([P, V_HALF, PACK], F32, name=f"both{h}", align_bytes=64) for h in range(2)]
+            nc.scalar.activation(first[h][:], dealt(banks_a[h][:]), COPY)
+        both = [keep.tile([V_HALF, 2, P, 2], F32, name=f"both{h}", align_bytes=64) for h in range(2)]
         for h in range(2):
-            nc.vector.tensor_tensor(both[h][:], product(1, h), first[h][:], MULT)
-        round_w(2, 0, 4)
-        round_w(2, 1, 1)
+            nc.vector.tensor_tensor(both[h][:], dealt(banks[h][:]), first[h][:], MULT)
 
-        w4_bf = keep.tile([P, N * PACK], BF16, name="w4_bf", align_bytes=64)
-        nc.scalar.activation(
-            w4_bf[:].rearrange("p (c i j) -> p c j i", i=4, j=PACK),
-            w4_raw[:].rearrange("p j (c i) -> p c j i", i=4),
-            COPY,
-        )
-        w4_words = keep.tile([P, N], U32, name="w4_words", align_bytes=64)
-        w4_scales = keep.tile([P, N], U8, name="w4_scales", align_bytes=64)
-        nc.vector.quantize_mx(out=w4_words[:].bitcast(FP8X4), scales=w4_scales[:], in_=w4_bf[:])
+        words, scales = weights("w20", w_raw[2, 0], (256, 256, 256)[0])
+        third = {}
+        for c in range(2):
+            cols = slice(c * H_HALF, (c + 1) * H_HALF)
+            for h in range(2):
+                third[c, h] = psum.tile([V_HALF, H_HALF], F32, name=f"third{c}{h}", tag=f"third{c}")
+                one_pass(third[c, h][:], 2, 0, h, words[:, cols], scales[:, cols])
+        z_rows = [keep.tile([V_HALF, 2, P, 2], BF16, name=f"z_rows{h}", align_bytes=64) for h in range(2)]
+        late = []
+        for c in range(2):
+            late.append(weights(f"w21{c}", w3_late[c], (256, 256, 256)[1 + c]))
+            for h in range(2):
+                one_pass(third[c, h][:], 2, 1, h, late[c][0][:], late[c][1][:])
+        w4_words, w4_scales = weights("w4", w4_raw, N)
+        for c in range(2):
+            part = slice(c * (P // 2), (c + 1) * (P // 2))
+            for h in range(2):
+                nc.vector.tensor_tensor(z_rows[h][:, :, part, :], dealt(third[c, h][:]), both[h][:, :, part, :], MULT)
 
-        z_bf = [keep.tile([P, V_HALF, PACK], BF16, name=f"z_bf{h}", align_bytes=64) for h in range(2)]
+        turned = []
         for h in range(2):
-            nc.vector.tensor_tensor(z_bf[h][:], product(2, h), both[h][:], MULT)
+            pairs = z_rows[h][:].rearrange("v u p e -> v (u p e)").bitcast(F32)
+            turned.append(psum.tile([P, 2, V_HALF], F32, name=f"turned{h}", tag="early"))
+            for u in range(2):
+                nc.tensor.transpose(turned[h][:, u, :], pairs[:, u * P : (u + 1) * P], identity[:])
+        z_packed = [keep.tile([P, V_HALF, 2], F32, name=f"z_packed{h}", align_bytes=64) for h in range(2)]
+        nc.scalar.copy(z_packed[0][:], turned[0][:].rearrange("p u v -> p v u"))
+        nc.vector.tensor_copy(z_packed[1][:], turned[1][:].rearrange("p u v -> p v u"))
         for h in range(2):
             z_words = keep.tile([P, V_HALF], U32, name=f"z_words{h}", align_bytes=64)
             z_scales = keep.tile([P, V_HALF], U8, name=f"z_scales{h}", align_bytes=64)
-            nc.vector.quantize_mx(
-                out=z_words[:].bitcast(FP8X4), scales=z_scales[:], in_=z_bf[h][:].rearrange("p v t -> p (v t)")
-            )
-            last = psum.tile([N, V_HALF], F32, name=f"last{h}")
+            quantize(z_words[:], z_scales[:], z_packed[h][:].rearrange("p v u -> p (v u)").bitcast(BF16))
+            last = psum.tile([N, V_HALF], F32, name=f"last{h}", tag="late")
             nc.tensor.matmul_mx(
                 out=last[:],
                 lhsT=w4_words[:].bitcast(FP8X4),

@@ -21,10 +21,14 @@ P = 128
 PACK = 4
 K_PASS = P * PACK
 PASSES = K // K_PASS
-T_HALF = T // 2
+RUN = 4
+T_HALF, T_QUARTER = T // 2, T // 4
 V_HALF = V // 2
 H_HALF = H // 2
-LIST_COLS = V // 16
+
+X_QUARTERS_ON_VECTOR = ((0, 0), (0, 1), (1, 0), (1, 1))
+W2_SCALAR_COLS = (384, 160)
+W3_SCALAR_COLS = 240
 
 
 def tile_picked_trilin_relu_e_kernel(tc, xT, w1, w2, w3, w4, offs, out):
@@ -33,7 +37,7 @@ def tile_picked_trilin_relu_e_kernel(tc, xT, w1, w2, w3, w4, offs, out):
         keep = ctx.enter_context(tc.tile_pool(name="keep", bufs=1))
         psum = ctx.enter_context(tc.psum_pool(name="psum", bufs=2))
 
-        offsets = keep.tile([P, PIECES * LIST_COLS], U16, name="offsets")
+        offsets = keep.tile([P, PIECES * V // 16], U16, name="offsets")
         x_scales = keep.tile([P, T], U8, name="x_scales", align_bytes=64)
         nc.gpsimd.memset(x_scales[:].bitcast(U32), 0)
         identity = keep.tile([P, P], F32, name="identity", align_bytes=64)
@@ -45,122 +49,137 @@ def tile_picked_trilin_relu_e_kernel(tc, xT, w1, w2, w3, w4, offs, out):
             nc.sync.dma_start(raw[:], rows[:, :, cols])
             return raw
 
-        def interleave(name, raw, scalar_cols):
+        def round_to_bf16(name, raw, scalar_cols):
             width = raw.shape[2]
-            packed = keep.tile([P, width * PACK], BF16, name=name, align_bytes=64)
-            dst = packed[:].rearrange("p (c i j) -> p c j i", i=4, j=PACK)
-            src = raw.rearrange("p j (c i) -> p c j i", i=4)
-            cut = (width - scalar_cols) // 4
+            rounded = keep.tile([P, width * PACK], BF16, name=name, align_bytes=64)
+            dst = rounded[:].rearrange("p (c i j) -> p c j i", i=RUN, j=PACK)
+            src = raw.rearrange("p j (c i) -> p c j i", i=RUN)
+            cut = (width - scalar_cols) // RUN
             if cut:
                 nc.vector.tensor_copy(dst[:, :cut], src[:, :cut])
             if scalar_cols:
                 nc.scalar.activation(dst[:, cut:], src[:, cut:], COPY)
-            return packed
+            return rounded
 
-        def quantize(words, scales, packed):
-            nc.vector.quantize_mx(out=words.bitcast(FP8X4), scales=scales, in_=packed)
+        def quantize(words, scales, rounded):
+            nc.vector.quantize_mx(out=words.bitcast(FP8X4), scales=scales, in_=rounded)
 
-        halves = [slice(0, T_HALF), slice(T_HALF, T)]
-        x_raw = {}
-        for g in range(PASSES):
-            for h in range(2):
-                x_raw[g, h] = load(f"x_raw{g}{h}", xT, g, halves[h])[:]
-                if (g, h) == (0, 0):
-                    nc.sync.dma_start(offsets[:], offs)
-        w_raw = {}
-        for d, matrix in enumerate((w1, w2, w3)):
-            w_raw[d, 0] = load(f"w_raw{d}0", matrix, 0, slice(0, H))
-            if d < PIECES - 1:
-                w_raw[d, 1] = load(f"w_raw{d}1", matrix, 1, slice(0, H))
-        w3_late = [load(f"w3_late{c}", w3, 1, slice(c * H_HALF, (c + 1) * H_HALF)) for c in range(2)]
+        x_whole = [load("x_raw0", xT, 0, slice(0, T))]
+        nc.sync.dma_start(offsets[:], offs)
+        x_whole.append(load("x_raw1", xT, 1, slice(0, T)))
+        x_raw = [[whole[:, :, q * T_QUARTER : (q + 1) * T_QUARTER] for q in range(4)] for whole in x_whole]
+        w1_raw = [load(f"w1_raw{g}", w1, g, slice(0, H)) for g in range(PASSES)]
+        w2_raw = [load(f"w2_raw{g}", w2, g, slice(0, H)) for g in range(PASSES)]
+        w3_first_raw = load("w3_first_raw", w3, 0, slice(0, H))
+        channel_halves = (slice(0, H_HALF), slice(H_HALF, H))
+        w3_last_raw = [load(f"w3_last_raw{c}", w3, 1, cols) for c, cols in enumerate(channel_halves)]
         w4_raw = load("w4_raw", w4, 0, slice(0, N))
 
-        x_words = [keep.tile([P, T], U32, name=f"x_words{g}", align_bytes=64) for g in range(PASSES)]
-        picked_words = {}
+        picked_words = []
         for g in range(PASSES):
-            for h in range(2):
-                packed = interleave(f"x_bf{g}{h}", x_raw[g, h], (176, 176, 512, 176)[2 * g + h])
-                quantize(x_words[g][:, halves[h]], x_scales[4 * g : P, halves[h]], packed[:])
-            picked_words[g] = keep.tile([P, PIECES * V], U32, name=f"picked_words{g}", align_bytes=64)
-            nc.vector.tensor_copy(picked_words[g][:], x_words[g][:].indirect(offsets[:]))
+            x_words = keep.tile([P, T], U32, name=f"x_words{g}", align_bytes=64)
+            for q in range(4):
+                cols = slice(q * T_QUARTER, (q + 1) * T_QUARTER)
+                scalar_cols = 0 if (g, q) in X_QUARTERS_ON_VECTOR else T_QUARTER
+                rounded = round_to_bf16(f"x_rounded{g}{q}", x_raw[g][q], scalar_cols)
+                quantize(x_words[:, cols], x_scales[4 * g : P, cols], rounded[:])
+            picked_words.append(keep.tile([P, PIECES * V], U32, name=f"picked_words{g}", align_bytes=64))
+            nc.vector.tensor_copy(picked_words[g][:], x_words[:].indirect(offsets[:]))
         picked_scales = keep.tile([P, PIECES * V], U8, name="picked_scales", align_bytes=64)
         nc.vector.tensor_copy(picked_scales[:], x_scales[:].indirect(offsets[:]))
 
-        def weights(name, raw, scalar_cols):
+        def quantize_weights(name, raw, scalar_cols, scales_tag=None):
             width = raw.shape[2]
-            packed = interleave(name + "_bf", raw[:], scalar_cols)
+            rounded = round_to_bf16(name + "_rounded", raw[:], scalar_cols)
             words = keep.tile([P, width], U32, name=name + "_words", align_bytes=64)
-            scales = keep.tile([P, width], U8, name=name + "_scales", align_bytes=64)
-            quantize(words[:], scales[:], packed[:])
-            return words, scales
+            scales = keep.tile([P, width], U8, name=name + "_scales", tag=scales_tag or name + "_scales", align_bytes=64)
+            quantize(words[:], scales[:], rounded[:])
+            return words, scales, rounded
 
-        def one_pass(bank, d, g, h, words, scales):
-            v_cols = slice(d * V + h * V_HALF, d * V + (h + 1) * V_HALF)
+        def multiply_pass(bank, d, g, h, words, scales):
+            entries = slice(d * V + h * V_HALF, d * V + (h + 1) * V_HALF)
             nc.tensor.matmul_mx(
                 out=bank,
-                lhsT=picked_words[g][:, v_cols].bitcast(FP8X4),
-                lhsT_scale=picked_scales[4 * g : P, v_cols],
+                lhsT=picked_words[g][:, entries].bitcast(FP8X4),
+                lhsT_scale=picked_scales[4 * g : P, entries],
                 rhs=words.bitcast(FP8X4),
                 rhs_scale=scales,
                 start=(g == 0),
                 stop=(g == PASSES - 1),
             )
 
-        def dealt(bank):
-            return bank.rearrange("v (p u e) -> v u p e", u=2, e=2)
-
-        def product(d, tag, shares):
-            banks = [psum.tile([V_HALF, H], F32, name=f"bank{d}{h}", tag=tag) for h in range(2)]
+        def product(d, raws, scalar_cols):
+            banks = [psum.tile([V_HALF, H], F32, name=f"product{d}{h}", tag=f"product{d}") for h in range(2)]
             for g in range(PASSES):
-                words, scales = weights(f"w{d}{g}", w_raw[d, g], shares[g])
+                words, scales, rounded = quantize_weights(f"w{d + 1}{g}", raws[g], scalar_cols[g])
                 for h in range(2):
-                    one_pass(banks[h][:], d, g, h, words[:], scales[:])
+                    multiply_pass(banks[h][:], d, g, h, words[:], scales[:])
             return banks
 
-        banks_a = product(0, "early", (512, 512))
-        banks = product(1, "late", (288, 176))
-        first = [keep.tile([V_HALF, 2, P, 2], F32, name=f"first{h}", align_bytes=64) for h in range(2)]
-        for h in range(2):
-            nc.scalar.activation(first[h][:], dealt(banks_a[h][:]), COPY)
-        both = [keep.tile([V_HALF, 2, P, 2], F32, name=f"both{h}", align_bytes=64) for h in range(2)]
-        for h in range(2):
-            nc.vector.tensor_tensor(both[h][:], dealt(banks[h][:]), first[h][:], MULT)
+        def by_pairs(bank):
+            return bank.rearrange("v (p u e) -> v u p e", u=2, e=2)
 
-        words, scales = weights("w20", w_raw[2, 0], (256, 256, 256)[0])
-        third = {}
-        for c in range(2):
-            cols = slice(c * H_HALF, (c + 1) * H_HALF)
-            for h in range(2):
-                third[c, h] = psum.tile([V_HALF, H_HALF], F32, name=f"third{c}{h}", tag=f"third{c}")
-                one_pass(third[c, h][:], 2, 0, h, words[:, cols], scales[:, cols])
-        z_rows = [keep.tile([V_HALF, 2, P, 2], BF16, name=f"z_rows{h}", align_bytes=64) for h in range(2)]
-        late = []
-        for c in range(2):
-            late.append(weights(f"w21{c}", w3_late[c], (256, 256, 256)[1 + c]))
-            for h in range(2):
-                one_pass(third[c, h][:], 2, 1, h, late[c][0][:], late[c][1][:])
-        w4_words, w4_scales = weights("w4", w4_raw, N)
-        for c in range(2):
-            part = slice(c * (P // 2), (c + 1) * (P // 2))
-            for h in range(2):
-                nc.vector.tensor_tensor(z_rows[h][:, :, part, :], dealt(third[c, h][:]), both[h][:, :, part, :], MULT)
+        def in_rows(view):
+            return view.rearrange("v u (a p) e -> v u a p e", a=2)
 
+        first_banks = product(0, w1_raw, (H, H))
+        second_banks = product(1, w2_raw, W2_SCALAR_COLS)
+
+        first = []
+        for h in range(2):
+            spent = w2_raw[PASSES - 1][:, :, H - (h + 1) * P : H - h * P]
+            first.append(spent.rearrange("v (u a) (p e) -> v u a p e", u=2, e=2))
+            nc.scalar.activation(first[h], in_rows(by_pairs(first_banks[h][:])), COPY)
+
+        w3_words, w3_scales, w3_first_rounded = quantize_weights("w3_first", w3_first_raw, W3_SCALAR_COLS)
+        third_banks = {}
+        for c, cols in enumerate(channel_halves):
+            for h in range(2):
+                third_banks[c, h] = psum.tile([V_HALF, H_HALF], F32, name=f"third{c}{h}", tag=f"third{c}")
+                multiply_pass(third_banks[c, h][:], 2, 0, h, w3_words[:, cols], w3_scales[:, cols])
+
+        w3_last_rounded = []
+        for c in range(2):
+            w3_words, w3_scales, rounded = quantize_weights(f"w3_last{c}", w3_last_raw[c], H_HALF)
+            w3_last_rounded.append(rounded)
+            for h in range(2):
+                multiply_pass(third_banks[c, h][:], 2, 1, h, w3_words[:], w3_scales[:])
+
+        both = [
+            w3_first_raw[:, 0:2, :H_HALF].rearrange("v u (p e) -> v u p e", e=2),
+            w3_first_rounded[:, : 2 * H].bitcast(F32).rearrange("v (u p e) -> v u p e", u=2, e=2),
+        ]
+        for h in range(2):
+            nc.vector.tensor_tensor(in_rows(both[h]), in_rows(by_pairs(second_banks[h][:])), first[h], MULT)
+
+        z_tile = w3_last_rounded[1]
+        z_rows = z_tile[:].rearrange("v (h u p e) -> v h u p e", h=2, u=2, e=2)
+        for c in range(2):
+            part = slice(c * P // 2, (c + 1) * P // 2)
+            for h in range(2):
+                nc.vector.tensor_tensor(
+                    z_rows[:, h, :, part, :], by_pairs(third_banks[c, h][:]), both[h][:, :, part, :], MULT
+                )
+
+        w4_words, w4_scales, rounded = quantize_weights("w4", w4_raw, N, "w3_first_rounded")
+
+        z_pairs = z_tile[:].bitcast(F32).rearrange("v (h u p) -> v h u p", h=2, u=2)
         turned = []
         for h in range(2):
-            pairs = z_rows[h][:].rearrange("v u p e -> v (u p e)").bitcast(F32)
-            turned.append(psum.tile([P, 2, V_HALF], F32, name=f"turned{h}", tag="early"))
+            turned.append(psum.tile([P, 2, V_HALF], F32, name=f"turned{h}", tag="product0"))
             for u in range(2):
-                nc.tensor.transpose(turned[h][:, u, :], pairs[:, u * P : (u + 1) * P], identity[:])
-        z_packed = [keep.tile([P, V_HALF, 2], F32, name=f"z_packed{h}", align_bytes=64) for h in range(2)]
-        nc.scalar.copy(z_packed[0][:], turned[0][:].rearrange("p u v -> p v u"))
-        nc.vector.tensor_copy(z_packed[1][:], turned[1][:].rearrange("p u v -> p v u"))
+                nc.tensor.transpose(turned[h][:, u, :], z_pairs[:, h, u, :], identity[:])
+        z_rounded = [keep.tile([P, V_HALF, 2], F32, name=f"z_rounded{h}", align_bytes=64) for h in range(2)]
+        nc.scalar.copy(z_rounded[0][:], turned[0][:].rearrange("p u v -> p v u"))
+        nc.vector.tensor_copy(z_rounded[1][:], turned[1][:].rearrange("p u v -> p v u"))
+
         for h in range(2):
             z_words = keep.tile([P, V_HALF], U32, name=f"z_words{h}", align_bytes=64)
             z_scales = keep.tile([P, V_HALF], U8, name=f"z_scales{h}", align_bytes=64)
-            quantize(z_words[:], z_scales[:], z_packed[h][:].rearrange("p v u -> p (v u)").bitcast(BF16))
-            last = psum.tile([N, V_HALF], F32, name=f"last{h}", tag="late")
+            quantize(z_words[:], z_scales[:], z_rounded[h][:].rearrange("p v u -> p (v u)").bitcast(BF16))
+            last_bank = psum.tile([N, V_HALF], F32, name=f"last{h}", tag="product1")
             nc.tensor.matmul_mx(
-                out=last[:],
+                out=last_bank[:],
                 lhsT=w4_words[:].bitcast(FP8X4),
                 lhsT_scale=w4_scales[:],
                 rhs=z_words[:].bitcast(FP8X4),
@@ -169,5 +188,5 @@ def tile_picked_trilin_relu_e_kernel(tc, xT, w1, w2, w3, w4, offs, out):
                 stop=True,
             )
             result = keep.tile([N, V_HALF], F32, name=f"result{h}", align_bytes=64)
-            nc.scalar.activation(result[:], last[:], RELU)
+            nc.scalar.activation(result[:], last_bank[:], RELU)
             nc.sync.dma_start(out[:, h * V_HALF : (h + 1) * V_HALF], result[:])

from contextlib import ExitStack

import concourse.mybir as mybir
from concourse.masks import make_identity

K, T, V, H, N = 1024, 1024, 256, 512, 128
PIECES = 3
FLOPS = 2 * PIECES * K * H * V + 2 * H * N * V

F32 = mybir.dt.float32
BF16 = mybir.dt.bfloat16
U32 = mybir.dt.uint32
U16 = mybir.dt.uint16
U8 = mybir.dt.uint8
FP8X4 = mybir.dt.float8_e4m3fn_x4
MULT = mybir.AluOpType.mult
COPY = mybir.ActivationFunctionType.Copy
RELU = mybir.ActivationFunctionType.Relu

P = 128
PACK = 4
K_PASS = P * PACK
PASSES = K // K_PASS
RUN = 4
T_HALF, T_QUARTER = T // 2, T // 4
V_HALF = V // 2
H_HALF = H // 2

X_QUARTERS_ON_VECTOR = ((0, 0), (0, 1), (1, 0), (1, 1))
W2_SCALAR_COLS = (384, 160)
W3_SCALAR_COLS = 240


def tile_picked_trilin_relu_e_kernel(tc, xT, w1, w2, w3, w4, offs, out):
    nc = tc.nc
    with ExitStack() as ctx:
        keep = ctx.enter_context(tc.tile_pool(name="keep", bufs=1))
        psum = ctx.enter_context(tc.psum_pool(name="psum", bufs=2))

        offsets = keep.tile([P, PIECES * V // 16], U16, name="offsets")
        x_scales = keep.tile([P, T], U8, name="x_scales", align_bytes=64)
        nc.gpsimd.memset(x_scales[:].bitcast(U32), 0)
        identity = keep.tile([P, P], F32, name="identity", align_bytes=64)
        make_identity(nc, identity[:])

        def load(name, matrix, g, cols):
            rows = matrix[g * K_PASS : (g + 1) * K_PASS, :].rearrange("(p j) c -> p j c", j=PACK)
            raw = keep.tile([P, PACK, cols.stop - cols.start], F32, name=name, align_bytes=64)
            nc.sync.dma_start(raw[:], rows[:, :, cols])
            return raw

        def round_to_bf16(name, raw, scalar_cols):
            width = raw.shape[2]
            rounded = keep.tile([P, width * PACK], BF16, name=name, align_bytes=64)
            dst = rounded[:].rearrange("p (c i j) -> p c j i", i=RUN, j=PACK)
            src = raw.rearrange("p j (c i) -> p c j i", i=RUN)
            cut = (width - scalar_cols) // RUN
            if cut:
                nc.vector.tensor_copy(dst[:, :cut], src[:, :cut])
            if scalar_cols:
                nc.scalar.activation(dst[:, cut:], src[:, cut:], COPY)
            return rounded

        def quantize(words, scales, rounded):
            nc.vector.quantize_mx(out=words.bitcast(FP8X4), scales=scales, in_=rounded)

        x_whole = [load("x_raw0", xT, 0, slice(0, T))]
        nc.sync.dma_start(offsets[:], offs)
        x_whole.append(load("x_raw1", xT, 1, slice(0, T)))
        x_raw = [[whole[:, :, q * T_QUARTER : (q + 1) * T_QUARTER] for q in range(4)] for whole in x_whole]
        w1_raw = [load(f"w1_raw{g}", w1, g, slice(0, H)) for g in range(PASSES)]
        w2_raw = [load(f"w2_raw{g}", w2, g, slice(0, H)) for g in range(PASSES)]
        w3_first_raw = load("w3_first_raw", w3, 0, slice(0, H))
        channel_halves = (slice(0, H_HALF), slice(H_HALF, H))
        w3_last_raw = [load(f"w3_last_raw{c}", w3, 1, cols) for c, cols in enumerate(channel_halves)]
        w4_raw = load("w4_raw", w4, 0, slice(0, N))

        picked_words = []
        for g in range(PASSES):
            x_words = keep.tile([P, T], U32, name=f"x_words{g}", align_bytes=64)
            for q in range(4):
                cols = slice(q * T_QUARTER, (q + 1) * T_QUARTER)
                scalar_cols = 0 if (g, q) in X_QUARTERS_ON_VECTOR else T_QUARTER
                rounded = round_to_bf16(f"x_rounded{g}{q}", x_raw[g][q], scalar_cols)
                quantize(x_words[:, cols], x_scales[4 * g : P, cols], rounded[:])
            picked_words.append(keep.tile([P, PIECES * V], U32, name=f"picked_words{g}", align_bytes=64))
            nc.vector.tensor_copy(picked_words[g][:], x_words[:].indirect(offsets[:]))
        picked_scales = keep.tile([P, PIECES * V], U8, name="picked_scales", align_bytes=64)
        nc.vector.tensor_copy(picked_scales[:], x_scales[:].indirect(offsets[:]))

        def quantize_weights(name, raw, scalar_cols, scales_tag=None):
            width = raw.shape[2]
            rounded = round_to_bf16(name + "_rounded", raw[:], scalar_cols)
            words = keep.tile([P, width], U32, name=name + "_words", align_bytes=64)
            scales = keep.tile([P, width], U8, name=name + "_scales", tag=scales_tag or name + "_scales", align_bytes=64)
            quantize(words[:], scales[:], rounded[:])
            return words, scales, rounded

        def multiply_pass(bank, d, g, h, words, scales):
            entries = slice(d * V + h * V_HALF, d * V + (h + 1) * V_HALF)
            nc.tensor.matmul_mx(
                out=bank,
                lhsT=picked_words[g][:, entries].bitcast(FP8X4),
                lhsT_scale=picked_scales[4 * g : P, entries],
                rhs=words.bitcast(FP8X4),
                rhs_scale=scales,
                start=(g == 0),
                stop=(g == PASSES - 1),
            )

        def product(d, raws, scalar_cols):
            banks = [psum.tile([V_HALF, H], F32, name=f"product{d}{h}", tag=f"product{d}") for h in range(2)]
            for g in range(PASSES):
                words, scales, rounded = quantize_weights(f"w{d + 1}{g}", raws[g], scalar_cols[g])
                for h in range(2):
                    multiply_pass(banks[h][:], d, g, h, words[:], scales[:])
            return banks

        def by_pairs(bank):
            return bank.rearrange("v (p u e) -> v u p e", u=2, e=2)

        def in_rows(view):
            return view.rearrange("v u (a p) e -> v u a p e", a=2)

        first_banks = product(0, w1_raw, (H, H))
        second_banks = product(1, w2_raw, W2_SCALAR_COLS)

        first = []
        for h in range(2):
            spent = w2_raw[PASSES - 1][:, :, H - (h + 1) * P : H - h * P]
            first.append(spent.rearrange("v (u a) (p e) -> v u a p e", u=2, e=2))
            nc.scalar.activation(first[h], in_rows(by_pairs(first_banks[h][:])), COPY)

        w3_words, w3_scales, w3_first_rounded = quantize_weights("w3_first", w3_first_raw, W3_SCALAR_COLS)
        third_banks = {}
        for c, cols in enumerate(channel_halves):
            for h in range(2):
                third_banks[c, h] = psum.tile([V_HALF, H_HALF], F32, name=f"third{c}{h}", tag=f"third{c}")
                multiply_pass(third_banks[c, h][:], 2, 0, h, w3_words[:, cols], w3_scales[:, cols])

        w3_last_rounded = []
        for c in range(2):
            w3_words, w3_scales, rounded = quantize_weights(f"w3_last{c}", w3_last_raw[c], H_HALF)
            w3_last_rounded.append(rounded)
            for h in range(2):
                multiply_pass(third_banks[c, h][:], 2, 1, h, w3_words[:], w3_scales[:])

        both = [
            w3_first_raw[:, 0:2, :H_HALF].rearrange("v u (p e) -> v u p e", e=2),
            w3_first_rounded[:, : 2 * H].bitcast(F32).rearrange("v (u p e) -> v u p e", u=2, e=2),
        ]
        for h in range(2):
            nc.vector.tensor_tensor(in_rows(both[h]), in_rows(by_pairs(second_banks[h][:])), first[h], MULT)

        z_tile = w3_last_rounded[1]
        z_rows = z_tile[:].rearrange("v (h u p e) -> v h u p e", h=2, u=2, e=2)
        for c in range(2):
            part = slice(c * P // 2, (c + 1) * P // 2)
            for h in range(2):
                nc.vector.tensor_tensor(
                    z_rows[:, h, :, part, :], by_pairs(third_banks[c, h][:]), both[h][:, :, part, :], MULT
                )

        w4_words, w4_scales, rounded = quantize_weights("w4", w4_raw, N, "w3_first_rounded")

        z_pairs = z_tile[:].bitcast(F32).rearrange("v (h u p) -> v h u p", h=2, u=2)
        turned = []
        for h in range(2):
            turned.append(psum.tile([P, 2, V_HALF], F32, name=f"turned{h}", tag="product0"))
            for u in range(2):
                nc.tensor.transpose(turned[h][:, u, :], z_pairs[:, h, u, :], identity[:])
        z_rounded = [keep.tile([P, V_HALF, 2], F32, name=f"z_rounded{h}", align_bytes=64) for h in range(2)]
        nc.scalar.copy(z_rounded[0][:], turned[0][:].rearrange("p u v -> p v u"))
        nc.vector.tensor_copy(z_rounded[1][:], turned[1][:].rearrange("p u v -> p v u"))

        for h in range(2):
            z_words = keep.tile([P, V_HALF], U32, name=f"z_words{h}", align_bytes=64)
            z_scales = keep.tile([P, V_HALF], U8, name=f"z_scales{h}", align_bytes=64)
            quantize(z_words[:], z_scales[:], z_rounded[h][:].rearrange("p v u -> p (v u)").bitcast(BF16))
            last_bank = psum.tile([N, V_HALF], F32, name=f"last{h}", tag="product1")
            nc.tensor.matmul_mx(
                out=last_bank[:],
                lhsT=w4_words[:].bitcast(FP8X4),
                lhsT_scale=w4_scales[:],
                rhs=z_words[:].bitcast(FP8X4),
                rhs_scale=z_scales[:],
                start=True,
                stop=True,
            )
            result = keep.tile([N, V_HALF], F32, name=f"result{h}", align_bytes=64)
            nc.scalar.activation(result[:], last_bank[:], RELU)
            nc.sync.dma_start(out[:, h * V_HALF : (h + 1) * V_HALF], result[:])
